import numpy as np
import ml_dtypes


def mxq(x, axis, fmt="e4m3"):
    dtype, down = {"e4m3": (ml_dtypes.float8_e4m3fn, 7), "e5m2": (ml_dtypes.float8_e5m2, 14)}[fmt]
    v = np.moveaxis(np.asarray(x, np.float32).astype(ml_dtypes.bfloat16).astype(np.float64), axis, -1)
    blocks = v.reshape(v.shape[:-1] + (-1, 32))
    amax = np.abs(blocks).max(-1, keepdims=True)
    byte = np.maximum(np.where(amax > 0, np.frexp(amax)[1] - 1 + 127, 0) - down, 1)
    scale = np.exp2(byte - 127.0)
    codes = (blocks / scale).astype(np.float32).astype(dtype).astype(np.float64)
    return np.moveaxis((codes * scale).reshape(v.shape), -1, axis)


WIDE = False


def mx_kscale(k):
    if not WIDE:
        return np.ones(k)
    levels = np.array([10, -10, 5, -5, 0])
    if k % 512:
        return np.exp2(np.random.permutation(np.resize(levels, k // 32))).repeat(32)
    a = np.empty((k // 512, 16))
    for p in range(k // 512):
        a[p, :8] = np.random.permutation(np.resize(levels, 8))
        for g in range(8):
            far = levels[np.abs(levels - a[p, g]) >= 10]
            a[p, g + 8] = far[np.random.randint(len(far))]
    return np.exp2(a.ravel()).repeat(32)


def f64(x):
    return np.asarray(x).astype(np.float64)


def striped8(idx):
    return np.asarray(idx).reshape(8, -1, 16).transpose(0, 2, 1).reshape(128, -1).astype(np.uint16)


def unstriped8(offs):
    return offs.reshape(8, 16, -1).transpose(0, 2, 1).reshape(8, -1).astype(np.int64)


def pick8(x, idx, run):
    r = np.arange(len(x))
    return x[r[:, None], idx[r % (8 * run) // run]]


E2M1 = np.array([0.0, 0.5, 1.0, 1.5, 2.0, 3.0, 4.0, 6.0, -0.0, -0.5, -1.0, -1.5, -2.0, -3.0, -4.0, -6.0])


def pack_weight(w, fmt):
    k, n = w.shape
    w = f64(np.asarray(w, np.float32).astype(ml_dtypes.bfloat16)).reshape(k // 32, 32, n)
    amax = np.abs(w).max(1)
    if fmt == "e4m3":
        byte = np.frexp(amax)[1] - 1 + 127 - 7
    else:
        mant, ex = np.frexp(amax / 6.0)
        byte = np.where(mant > 0.5, ex, ex - 1) + 127
    byte = np.clip(np.where(amax > 0, byte, 1), 1, 254)
    scaled = (w * np.exp2(127.0 - byte)[:, None, :]).reshape(k, n).astype(np.float32)
    by_word = np.ascontiguousarray(scaled.reshape(k // 512, 128, 4, n).transpose(0, 1, 3, 2))
    if fmt == "e4m3":
        words = by_word.astype(ml_dtypes.float8_e4m3fn).view(np.uint8)
    else:
        c = by_word.astype(ml_dtypes.float4_e2m1fn).view(np.uint8) & 0xF
        words = (c[..., 0::2] | (c[..., 1::2] << 4)).reshape(k // 512, 128, 2 * n)
    return np.ascontiguousarray(words), np.ascontiguousarray(byte.astype(np.uint8).reshape(k // 512, 16, n))


def unpack_weight(words, scales, fmt):
    g, _, n = scales.shape
    words = np.ascontiguousarray(words).reshape(g, 128, n, -1)
    if fmt == "e4m3":
        vals = words.view(ml_dtypes.float8_e4m3fn).astype(np.float64)
    else:
        nib = np.empty((g, 128, n, 4), np.uint8)
        nib[..., 0::2] = words & 0xF
        nib[..., 1::2] = words >> 4
        vals = E2M1[nib]
    vals = vals * np.repeat(np.exp2(scales.astype(np.float64) - 127.0), 8, axis=1)[..., None]
    return vals.transpose(0, 1, 3, 2).reshape(g * 512, n)


D, K, T, U, X, I, Q = 512, 512, 1024, 1024, 1024, 512, 128


def setup_inputs():
    n = np.random.standard_normal
    idx = np.stack([np.random.permutation(T)[:I] for _ in range(8)])
    idx2 = np.stack([np.random.permutation(U)[:I] for _ in range(8)])
    idx3 = np.stack([np.random.permutation(X)[:I] for _ in range(8)])
    idx4 = np.stack([np.random.permutation(U)[:I] for _ in range(8)])
    idx5 = np.stack([np.random.permutation(T)[:I] for _ in range(8)])
    idx6 = np.stack([np.random.permutation(T)[:I] for _ in range(8)])
    idx7 = np.stack([np.random.permutation(X)[:I] for _ in range(8)])
    fd = mx_kscale(D)
    fk = mx_kscale(K)
    wqp = pack_weight(n((D, K)) * 1.0 / np.sqrt(D) * fd[:, None] * fk, "e4m3")
    cachep = pack_weight(n((K, T)) * 1.0 / np.sqrt(K) / fk[:, None], "e4m3")
    draftp = pack_weight(n((K, U)) * 1.0 / np.sqrt(K) / fk[:, None], "e2m1")
    archp = pack_weight(n((D, X)) * 1.0 / np.sqrt(D) * fd[:, None], "e4m3")
    return {
        "states": (n((D, Q)) * 0.95 / fd[:, None]).astype(np.float32),
        "wq_words": wqp[0],
        "wq_scales": wqp[1],
        "cache_words": cachep[0],
        "cache_scales": cachep[1],
        "draft_words": draftp[0],
        "draft_scales": draftp[1],
        "arch_words": archp[0],
        "arch_scales": archp[1],
        "offs": striped8(idx),
        "offs2": striped8(idx2),
        "offs3": striped8(idx3),
        "offs4": striped8(idx4),
        "offs5": striped8(idx5),
        "offs6": striped8(idx6),
        "offs7": striped8(idx7),
    }


def reference(states, wq_words, wq_scales, cache_words, cache_scales, draft_words, draft_scales, arch_words, arch_scales, offs, offs2, offs3, offs4, offs5, offs6, offs7):
    idx = unstriped8(offs)
    idx2 = unstriped8(offs2)
    idx3 = unstriped8(offs3)
    idx4 = unstriped8(offs4)
    idx5 = unstriped8(offs5)
    idx6 = unstriped8(offs6)
    idx7 = unstriped8(offs7)
    wqu = unpack_weight(wq_words, wq_scales, "e4m3")
    cacheu = unpack_weight(cache_words, cache_scales, "e4m3")
    draftu = unpack_weight(draft_words, draft_scales, "e2m1")
    archu = unpack_weight(arch_words, arch_scales, "e4m3")
    statesq = mxq(f64(states), 0, "e4m3")
    qv = wqu.T @ statesq
    qvq = mxq(qv, 0, "e4m3")
    a = qvq.T @ cacheu
    b = qvq.T @ draftu
    c0 = statesq.T @ archu
    f1 = np.zeros((Q, U))
    f1[np.arange(Q)[:, None], idx2[np.arange(Q) % 128 // 16]] = pick8(a, idx, 16)
    f2 = np.zeros((Q, X))
    f2[np.arange(Q)[:, None], idx3[np.arange(Q) % 128 // 16]] = pick8(a, idx, 16)
    bb = b + f1
    cc = c0 - f2
    f3 = np.zeros((Q, T))
    f3[np.arange(Q)[:, None], idx5[np.arange(Q) % 128 // 16]] = pick8(bb, idx4, 16)
    aa = a - f3
    y = np.maximum(pick8(aa, idx6, 16), pick8(cc, idx7, 16))
    return y

@@ -1,0 +1,183 @@
+from contextlib import ExitStack
+
+import concourse.mybir as mybir
+
+D, K, T, U, X, I, Q = 512, 512, 1024, 1024, 1024, 512, 128
+FLOPS = 2 * Q * (D * K + K * T + K * U + D * X)
+
+F32 = mybir.dt.float32
+BF16 = mybir.dt.bfloat16
+I32 = mybir.dt.int32
+U32 = mybir.dt.uint32
+U16 = mybir.dt.uint16
+U8 = mybir.dt.uint8
+FP8X4 = mybir.dt.float8_e4m3fn_x4
+FP4X4 = mybir.dt.float4_e2m1fn_x4
+COPY = mybir.ActivationFunctionType.Copy
+ADD = mybir.AluOpType.add
+SUB = mybir.AluOpType.subtract
+MAX = mybir.AluOpType.max
+
+P = 128
+PACK = 4
+BANK = 512
+A_PIECE = 256
+HALF = I // 2
+FILL = 64
+Q_VEC = 96
+PER_COL = 16
+
+
+def tile_attend_fanout_sidethree_kernel(tc, states, wq_words, wq_scales, cache_words, cache_scales, draft_words,
+                                         draft_scales, arch_words, arch_scales, offs, offs2, offs3, offs4, offs5,
+                                         offs6, offs7, out):
+    nc = tc.nc
+    with ExitStack() as ctx:
+        sb = ctx.enter_context(tc.tile_pool(name="sb", bufs=1))
+        ps = ctx.enter_context(tc.psum_pool(name="ps", bufs=1))
+
+        def tile(name, shape, dtype, tag=None):
+            return sb.tile(shape, dtype, name=name, tag=tag or name, align_bytes=64)
+
+        def load_words(name, words, tag=None):
+            t = tile(name, [P, words.shape[2]], U32, tag)
+            nc.sync.dma_start(t[:].bitcast(I32), words[0].rearrange("p n t -> p (n t)").bitcast(I32))
+            return t
+
+        def zeroed_plane(name, width, tag=None):
+            t = tile(name, [P, width], U8, tag)
+            nc.vector.memset(t[:].bitcast(I32), 0)
+            return t
+
+        def load_plane(plane, scales):
+            rows = scales[0].rearrange("(g r) n -> r g n", r=4)
+            for r in range(4):
+                nc.sync.dma_start(plane[r:P:32, :].bitcast(I32), rows[r].bitcast(I32))
+
+        def load_list(name, lst):
+            t = sb.tile([P, I // PER_COL], U16, name=name)
+            nc.sync.dma_start(t[:], lst)
+            return t
+
+        def entries(lst, lo, hi):
+            return lst[:, lo // PER_COL:hi // PER_COL]
+
+        wq_plane_raw = zeroed_plane("wq_plane_raw", K, tag="wq_plane_raw_then_f2")
+        cache_plane = zeroed_plane("cache_plane", T)
+        draft_plane = zeroed_plane("draft_plane", U)
+        arch_plane = zeroed_plane("arch_plane", X)
+        f1 = tile("f1", [P, U], F32)
+        nc.vector.memset(f1[:], 0.0)
+
+        st_raw = tile("st_raw", [P, PACK, Q], F32)
+        nc.sync.dma_start(st_raw[:], states.rearrange("(p j) q -> p j q", j=PACK))
+        wq_raw = load_words("wq_raw", wq_words)
+        load_plane(wq_plane_raw, wq_scales)
+        cache_w = load_words("cache_w", cache_words)
+        load_plane(cache_plane, cache_scales)
+        l1 = load_list("l1", offs)
+        l2 = load_list("l2", offs2)
+        l3 = load_list("l3", offs3)
+        draft_w = tile("draft_w", [P, 2 * U], U8, tag="draft_w_then_f3")
+        nc.sync.dma_start(draft_w[:].bitcast(I32), draft_words[0].bitcast(I32))
+        load_plane(draft_plane, draft_scales)
+        l4 = load_list("l4", offs4)
+        l5 = load_list("l5", offs5)
+        arch_w = load_words("arch_w", arch_words)
+        load_plane(arch_plane, arch_scales)
+        l7 = load_list("l7", offs7)
+        l6 = load_list("l6", offs6)
+
+        st_bf = tile("st_bf", [P, Q, PACK], BF16)
+        nc.vector.tensor_copy(st_bf[:, 0:Q_VEC, :].rearrange("p (c i) j -> p c j i", i=4),
+                              st_raw[:, :, 0:Q_VEC].rearrange("p j (c i) -> p c j i", i=4))
+        nc.scalar.activation(st_bf[:, Q_VEC:Q, :].rearrange("p (c i) j -> p c j i", i=4),
+                             st_raw[:, :, Q_VEC:Q].rearrange("p j (c i) -> p c j i", i=4), COPY)
+        st_w = tile("st_w", [P, Q], U32)
+        st_plane = tile("st_plane", [P, Q], U8)
+        nc.vector.quantize_mx(out=st_w[:].bitcast(FP8X4), scales=st_plane[:], in_=st_bf[:].rearrange("p q j -> p (q j)"))
+
+        wq_w = tile("wq_w", [P, K], U32)
+        nc.scalar.copy(wq_w[:].rearrange("p (t m) -> p m t", t=PACK), wq_raw[:].rearrange("p (m t) -> p m t", t=PACK))
+        wq_plane = tile("wq_plane", [P, K], U8)
+        nc.vector.tensor_copy(wq_plane[:].rearrange("p (t m) -> p t m", t=PACK),
+                              wq_plane_raw[:].rearrange("p (m t) -> p t m", t=PACK))
+        f2 = tile("f2", [P, X], F32, tag="wq_plane_raw_then_f2")
+        nc.vector.memset(f2[:], 0.0)
+
+        qv_ps = ps.tile([P, PACK, Q], F32, name="qv_ps")
+        for t in range(PACK):
+            cols = slice(t * P, (t + 1) * P)
+            nc.tensor.matmul_mx(out=qv_ps[:, t, :], lhsT=wq_w[:, cols].bitcast(FP8X4), lhsT_scale=wq_plane[:, cols],
+                                rhs=st_w[:].bitcast(FP8X4), rhs_scale=st_plane[:], start=True, stop=True)
+        qv_bf = tile("qv_bf", [P, Q, PACK], BF16)
+        nc.scalar.copy(qv_bf[:], qv_ps[:].rearrange("p t q -> p q t"))
+        qv_w = tile("qv_w", [P, Q], U32)
+        qv_plane = tile("qv_plane", [P, Q], U8)
+        nc.vector.quantize_mx(out=qv_w[:].bitcast(FP8X4), scales=qv_plane[:], in_=qv_bf[:].rearrange("p q t -> p (q t)"))
+
+        a = tile("a", [P, T], F32)
+        a_ps = []
+        for n in range(T // A_PIECE):
+            cols = slice(n * A_PIECE, (n + 1) * A_PIECE)
+            bank = ps.tile([P, A_PIECE], F32, name=f"a_ps{n}")
+            nc.tensor.matmul_mx(out=bank[:], lhsT=qv_w[:].bitcast(FP8X4), lhsT_scale=qv_plane[:],
+                                rhs=cache_w[:, cols].bitcast(FP8X4), rhs_scale=cache_plane[:, cols],
+                                start=True, stop=True)
+            if n % 2 == 1:
+                nc.scalar.copy(a[:, cols], bank[:])
+            else:
+                nc.vector.tensor_copy(a[:, cols], bank[:])
+            a_ps.append(bank)
+
+        def scatter(window, lst, src, lo, hi):
+            nc.scalar.activation(window[:].indirect(entries(lst, lo, hi)), src[:, lo:hi], COPY)
+
+        ga = tile("ga", [P, I], F32)
+        nc.vector.tensor_copy(ga[:, 0:HALF], a[:].indirect(entries(l1, 0, HALF)))
+        scatter(f1, l2, ga, 0, HALF)
+        scatter(f2, l3, ga, 0, FILL)
+        nc.vector.tensor_copy(ga[:, HALF:I], a[:].indirect(entries(l1, HALF, I)))
+        scatter(f1, l2, ga, HALF, I)
+        scatter(f2, l3, ga, FILL, I)
+
+        bb = tile("bb", [P, U], F32, tag="bb_cc_aa")
+        for n in range(U // BANK):
+            cols = slice(n * BANK, (n + 1) * BANK)
+            b_ps = ps.tile([P, BANK], F32, name=f"b_ps{n}", tag=f"b_then_c{n}")
+            nc.tensor.matmul_mx(out=b_ps[:], lhsT=qv_w[:].bitcast(FP8X4), lhsT_scale=qv_plane[:],
+                                rhs=draft_w[:, 2 * n * BANK:2 * (n + 1) * BANK].bitcast(FP4X4),
+                                rhs_scale=draft_plane[:, cols], start=True, stop=True)
+            nc.vector.tensor_tensor(bb[:, cols], b_ps[:], f1[:, cols], ADD)
+        f3 = tile("f3", [P, T], F32, tag="draft_w_then_f3")
+        nc.gpsimd.memset(f3[:], 0.0)
+        gb = tile("gb", [P, I], F32)
+        nc.vector.tensor_copy(gb[:], bb[:].indirect(l4[:]))
+        scatter(f3, l5, gb, 0, I)
+
+        cc = tile("cc", [P, X], F32, tag="bb_cc_aa")
+        for n in range(X // BANK):
+            cols = slice(n * BANK, (n + 1) * BANK)
+            c_ps = ps.tile([P, BANK], F32, name=f"c_ps{n}", tag=f"b_then_c{n}")
+            nc.tensor.matmul_mx(out=c_ps[:], lhsT=st_w[:].bitcast(FP8X4), lhsT_scale=st_plane[:],
+                                rhs=arch_w[:, cols].bitcast(FP8X4), rhs_scale=arch_plane[:, cols],
+                                start=True, stop=True)
+            nc.vector.tensor_tensor(cc[:, cols], c_ps[:], f2[:, cols], SUB)
+        gc = tile("gc", [P, I], F32)
+        nc.vector.tensor_copy(gc[:], cc[:].indirect(l7[:]))
+
+        aa = tile("aa", [P, T], F32, tag="bb_cc_aa")
+        last = T // A_PIECE - 1
+        for n in range(last):
+            cols = slice(n * A_PIECE, (n + 1) * A_PIECE)
+            nc.vector.tensor_tensor(aa[:, cols], a_ps[n][:], f3[:, cols], SUB)
+        cols = slice(last * A_PIECE, T)
+        nc.gpsimd.tensor_tensor(aa[:, cols], a[:, cols], f3[:, cols], SUB)
+
+        gaa = tile("gaa", [P, I], F32)
+        y = tile("y", [P, I], F32)
+        nc.vector.tensor_copy(gaa[:, 0:HALF], aa[:].indirect(entries(l6, 0, HALF)))
+        nc.scalar.activation(gaa[:, HALF:I], aa[:].indirect(entries(l6, HALF, I)), COPY)
+        for cols in (slice(0, HALF), slice(HALF, I)):
+            nc.vector.tensor_tensor(y[:, cols], gaa[:, cols], gc[:, cols], MAX)
+            nc.sync.dma_start(out[:, cols], y[:, cols])

@@ -21,9 +21,10 @@ MAX = mybir.AluOpType.max
 P = 128
 PACK = 4
 BANK = 512
-A_PIECE = 256
+A_EDGES = (0, 256, 512, 768, 896, 1024)
+A_ON_VECTOR = (0, 2)
+AA_SPLIT = 704
 HALF = I // 2
-FILL = 64
 Q_VEC = 96
 PER_COL = 16
 
@@ -62,23 +63,29 @@ def tile_attend_fanout_sidethree_kernel(tc, states, wq_words, wq_scales, cache_w
         def entries(lst, lo, hi):
             return lst[:, lo // PER_COL:hi // PER_COL]
 
-        wq_plane_raw = zeroed_plane("wq_plane_raw", K, tag="wq_plane_raw_then_f2")
+        wq_plane_raw = zeroed_plane("wq_plane_raw", K, tag="wq_plane_raw_then_f1b")
         cache_plane = zeroed_plane("cache_plane", T)
-        draft_plane = zeroed_plane("draft_plane", U)
+        draft_plane = zeroed_plane("draft_plane", U, tag="draft_plane_then_f3")
         arch_plane = zeroed_plane("arch_plane", X)
         f1 = tile("f1", [P, U], F32)
         nc.vector.memset(f1[:], 0.0)
 
         st_raw = tile("st_raw", [P, PACK, Q], F32)
         nc.sync.dma_start(st_raw[:], states.rearrange("(p j) q -> p j q", j=PACK))
-        wq_raw = load_words("wq_raw", wq_words)
-        load_plane(wq_plane_raw, wq_scales)
+        wq_src = wq_words[0].rearrange("p n t -> p (n t)").bitcast(I32)
+        wq_raw = []
+        for h in range(2):
+            half = tile(f"wq_raw{h}", [P, K // 2], U32)
+            nc.sync.dma_start(half[:].bitcast(I32), wq_src[:, h * (K // 2):(h + 1) * (K // 2)])
+            wq_raw.append(half)
+            if h == 0:
+                load_plane(wq_plane_raw, wq_scales)
         cache_w = load_words("cache_w", cache_words)
         load_plane(cache_plane, cache_scales)
         l1 = load_list("l1", offs)
         l2 = load_list("l2", offs2)
         l3 = load_list("l3", offs3)
-        draft_w = tile("draft_w", [P, 2 * U], U8, tag="draft_w_then_f3")
+        draft_w = tile("draft_w", [P, 2 * U], U8, tag="draft_w_then_f2")
         nc.sync.dma_start(draft_w[:].bitcast(I32), draft_words[0].bitcast(I32))
         load_plane(draft_plane, draft_scales)
         l4 = load_list("l4", offs4)
@@ -98,36 +105,43 @@ def tile_attend_fanout_sidethree_kernel(tc, states, wq_words, wq_scales, cache_w
         nc.vector.quantize_mx(out=st_w[:].bitcast(FP8X4), scales=st_plane[:], in_=st_bf[:].rearrange("p q j -> p (q j)"))
 
         wq_w = tile("wq_w", [P, K], U32)
-        nc.scalar.copy(wq_w[:].rearrange("p (t m) -> p m t", t=PACK), wq_raw[:].rearrange("p (m t) -> p m t", t=PACK))
+        for h in range(2):
+            nc.scalar.copy(wq_w[:].rearrange("p (t m) -> p m t", t=PACK)[:, h * (P // 2):(h + 1) * (P // 2), :],
+                           wq_raw[h][:].rearrange("p (m t) -> p m t", t=PACK))
         wq_plane = tile("wq_plane", [P, K], U8)
-        nc.vector.tensor_copy(wq_plane[:].rearrange("p (t m) -> p t m", t=PACK),
-                              wq_plane_raw[:].rearrange("p (m t) -> p t m", t=PACK))
-        f2 = tile("f2", [P, X], F32, tag="wq_plane_raw_then_f2")
-        nc.vector.memset(f2[:], 0.0)
+        for u in range(2):
+            nc.vector.tensor_copy(wq_plane[:].rearrange("p (t m) -> p t m", t=PACK)[:, 2 * u:2 * u + 2, :],
+                                  wq_plane_raw[:].rearrange("p (m t) -> p t m", t=PACK)[:, 2 * u:2 * u + 2, :])
+        f1b = tile("f1b", [P, U], F32, tag="wq_plane_raw_then_f1b")
+        nc.vector.memset(f1b[:], 0.0)
 
-        qv_ps = ps.tile([P, PACK, Q], F32, name="qv_ps")
-        for t in range(PACK):
-            cols = slice(t * P, (t + 1) * P)
-            nc.tensor.matmul_mx(out=qv_ps[:, t, :], lhsT=wq_w[:, cols].bitcast(FP8X4), lhsT_scale=wq_plane[:, cols],
-                                rhs=st_w[:].bitcast(FP8X4), rhs_scale=st_plane[:], start=True, stop=True)
         qv_bf = tile("qv_bf", [P, Q, PACK], BF16)
-        nc.scalar.copy(qv_bf[:], qv_ps[:].rearrange("p t q -> p q t"))
+        for u in range(2):
+            qv_ps = ps.tile([P, 2, Q], F32, name=f"qv_ps{u}", tag=f"qv_b_c{u}")
+            for e in range(2):
+                cols = slice((2 * u + e) * P, (2 * u + e + 1) * P)
+                nc.tensor.matmul_mx(out=qv_ps[:, e, :], lhsT=wq_w[:, cols].bitcast(FP8X4), lhsT_scale=wq_plane[:, cols],
+                                    rhs=st_w[:].bitcast(FP8X4), rhs_scale=st_plane[:], start=True, stop=True)
+            if u == 0:
+                nc.vector.tensor_copy(qv_bf[:, :, 0:2], qv_ps[:].rearrange("p e q -> p q e"))
+            else:
+                nc.scalar.copy(qv_bf[:, :, 2:4], qv_ps[:].rearrange("p e q -> p q e"))
         qv_w = tile("qv_w", [P, Q], U32)
         qv_plane = tile("qv_plane", [P, Q], U8)
         nc.vector.quantize_mx(out=qv_w[:].bitcast(FP8X4), scales=qv_plane[:], in_=qv_bf[:].rearrange("p q t -> p (q t)"))
 
         a = tile("a", [P, T], F32)
         a_ps = []
-        for n in range(T // A_PIECE):
-            cols = slice(n * A_PIECE, (n + 1) * A_PIECE)
-            bank = ps.tile([P, A_PIECE], F32, name=f"a_ps{n}")
+        for n in range(len(A_EDGES) - 1):
+            cols = slice(A_EDGES[n], A_EDGES[n + 1])
+            bank = ps.tile([P, cols.stop - cols.start], F32, name=f"a_ps{n}")
             nc.tensor.matmul_mx(out=bank[:], lhsT=qv_w[:].bitcast(FP8X4), lhsT_scale=qv_plane[:],
                                 rhs=cache_w[:, cols].bitcast(FP8X4), rhs_scale=cache_plane[:, cols],
                                 start=True, stop=True)
-            if n % 2 == 1:
-                nc.scalar.copy(a[:, cols], bank[:])
-            else:
+            if n in A_ON_VECTOR:
                 nc.vector.tensor_copy(a[:, cols], bank[:])
+            else:
+                nc.scalar.copy(a[:, cols], bank[:])
             a_ps.append(bank)
 
         def scatter(window, lst, src, lo, hi):
@@ -136,21 +150,24 @@ def tile_attend_fanout_sidethree_kernel(tc, states, wq_words, wq_scales, cache_w
         ga = tile("ga", [P, I], F32)
         nc.vector.tensor_copy(ga[:, 0:HALF], a[:].indirect(entries(l1, 0, HALF)))
         scatter(f1, l2, ga, 0, HALF)
-        scatter(f2, l3, ga, 0, FILL)
         nc.vector.tensor_copy(ga[:, HALF:I], a[:].indirect(entries(l1, HALF, I)))
-        scatter(f1, l2, ga, HALF, I)
-        scatter(f2, l3, ga, FILL, I)
+        scatter(f1b, l2, ga, HALF, I)
 
-        bb = tile("bb", [P, U], F32, tag="bb_cc_aa")
+        bb_half = tile("bb_half", [P, U], F32)
         for n in range(U // BANK):
             cols = slice(n * BANK, (n + 1) * BANK)
-            b_ps = ps.tile([P, BANK], F32, name=f"b_ps{n}", tag=f"b_then_c{n}")
+            b_ps = ps.tile([P, BANK], F32, name=f"b_ps{n}", tag=f"qv_b_c{n}")
             nc.tensor.matmul_mx(out=b_ps[:], lhsT=qv_w[:].bitcast(FP8X4), lhsT_scale=qv_plane[:],
                                 rhs=draft_w[:, 2 * n * BANK:2 * (n + 1) * BANK].bitcast(FP4X4),
                                 rhs_scale=draft_plane[:, cols], start=True, stop=True)
-            nc.vector.tensor_tensor(bb[:, cols], b_ps[:], f1[:, cols], ADD)
-        f3 = tile("f3", [P, T], F32, tag="draft_w_then_f3")
+            nc.vector.tensor_tensor(bb_half[:, cols], b_ps[:], f1[:, cols], ADD)
+        f2 = tile("f2", [P, X], F32, tag="draft_w_then_f2")
+        nc.gpsimd.memset(f2[:], 0.0)
+        f3 = tile("f3", [P, T], F32, tag="draft_plane_then_f3")
         nc.gpsimd.memset(f3[:], 0.0)
+        scatter(f2, l3, ga, 0, I)
+        bb = tile("bb", [P, U], F32, tag="bb_cc_aa")
+        nc.vector.tensor_tensor(bb[:], bb_half[:], f1b[:], ADD)
         gb = tile("gb", [P, I], F32)
         nc.vector.tensor_copy(gb[:], bb[:].indirect(l4[:]))
         scatter(f3, l5, gb, 0, I)
@@ -158,7 +175,7 @@ def tile_attend_fanout_sidethree_kernel(tc, states, wq_words, wq_scales, cache_w
         cc = tile("cc", [P, X], F32, tag="bb_cc_aa")
         for n in range(X // BANK):
             cols = slice(n * BANK, (n + 1) * BANK)
-            c_ps = ps.tile([P, BANK], F32, name=f"c_ps{n}", tag=f"b_then_c{n}")
+            c_ps = ps.tile([P, BANK], F32, name=f"c_ps{n}", tag=f"qv_b_c{n}")
             nc.tensor.matmul_mx(out=c_ps[:], lhsT=st_w[:].bitcast(FP8X4), lhsT_scale=st_plane[:],
                                 rhs=arch_w[:, cols].bitcast(FP8X4), rhs_scale=arch_plane[:, cols],
                                 start=True, stop=True)
@@ -167,17 +184,16 @@ def tile_attend_fanout_sidethree_kernel(tc, states, wq_words, wq_scales, cache_w
         nc.vector.tensor_copy(gc[:], cc[:].indirect(l7[:]))
 
         aa = tile("aa", [P, T], F32, tag="bb_cc_aa")
-        last = T // A_PIECE - 1
-        for n in range(last):
-            cols = slice(n * A_PIECE, (n + 1) * A_PIECE)
-            nc.vector.tensor_tensor(aa[:, cols], a_ps[n][:], f3[:, cols], SUB)
-        cols = slice(last * A_PIECE, T)
-        nc.gpsimd.tensor_tensor(aa[:, cols], a[:, cols], f3[:, cols], SUB)
+        for n, bank in enumerate(a_ps):
+            lo, hi = A_EDGES[n], min(A_EDGES[n + 1], AA_SPLIT)
+            if lo < hi:
+                nc.vector.tensor_tensor(aa[:, lo:hi], bank[:, 0:hi - lo], f3[:, lo:hi], SUB)
+        nc.gpsimd.tensor_tensor(aa[:, AA_SPLIT:T], a[:, AA_SPLIT:T], f3[:, AA_SPLIT:T], SUB)
 
         gaa = tile("gaa", [P, I], F32)
-        y = tile("y", [P, I], F32)
         nc.vector.tensor_copy(gaa[:, 0:HALF], aa[:].indirect(entries(l6, 0, HALF)))
         nc.scalar.activation(gaa[:, HALF:I], aa[:].indirect(entries(l6, HALF, I)), COPY)
-        for cols in (slice(0, HALF), slice(HALF, I)):
-            nc.vector.tensor_tensor(y[:, cols], gaa[:, cols], gc[:, cols], MAX)
-            nc.sync.dma_start(out[:, cols], y[:, cols])
+        for name, cols, tag in (("y_hi", slice(HALF, I), None), ("y_lo", slice(0, HALF), "bb_cc_aa")):
+            y = tile(name, [P, HALF], F32, tag)
+            nc.vector.tensor_tensor(y[:], gaa[:, cols], gc[:, cols], MAX)
+            nc.sync.dma_start(out[:, cols], y[:])

@@ -25,7 +25,7 @@ A_EDGES = (0, 256, 512, 768, 896, 1024)
 A_ON_VECTOR = (0, 2)
 AA_SPLIT = 704
 HALF = I // 2
-Q_VEC = 96
+Q_VEC = 80
 PER_COL = 16
 
 
@@ -63,7 +63,7 @@ def tile_attend_fanout_sidethree_kernel(tc, states, wq_words, wq_scales, cache_w
         def entries(lst, lo, hi):
             return lst[:, lo // PER_COL:hi // PER_COL]
 
-        wq_plane_raw = zeroed_plane("wq_plane_raw", K, tag="wq_plane_raw_then_f1b")
+        wq_plane_raw = zeroed_plane("wq_plane_raw", K)
         cache_plane = zeroed_plane("cache_plane", T)
         draft_plane = zeroed_plane("draft_plane", U, tag="draft_plane_then_f3")
         arch_plane = zeroed_plane("arch_plane", X)
@@ -105,17 +105,15 @@ def tile_attend_fanout_sidethree_kernel(tc, states, wq_words, wq_scales, cache_w
         nc.vector.quantize_mx(out=st_w[:].bitcast(FP8X4), scales=st_plane[:], in_=st_bf[:].rearrange("p q j -> p (q j)"))
 
         wq_w = tile("wq_w", [P, K], U32)
-        for h in range(2):
-            nc.scalar.copy(wq_w[:].rearrange("p (t m) -> p m t", t=PACK)[:, h * (P // 2):(h + 1) * (P // 2), :],
-                           wq_raw[h][:].rearrange("p (m t) -> p m t", t=PACK))
+        for h, places in ((0, slice(0, 4)), (1, slice(0, 2)), (1, slice(2, 4))):
+            nc.scalar.copy(wq_w[:].rearrange("p (t m) -> p m t", t=PACK)[:, h * (P // 2):(h + 1) * (P // 2), places],
+                           wq_raw[h][:].rearrange("p (m t) -> p m t", t=PACK)[:, :, places])
         wq_plane = tile("wq_plane", [P, K], U8)
         for u in range(2):
             nc.vector.tensor_copy(wq_plane[:].rearrange("p (t m) -> p t m", t=PACK)[:, 2 * u:2 * u + 2, :],
                                   wq_plane_raw[:].rearrange("p (m t) -> p t m", t=PACK)[:, 2 * u:2 * u + 2, :])
-        f1b = tile("f1b", [P, U], F32, tag="wq_plane_raw_then_f1b")
-        nc.vector.memset(f1b[:], 0.0)
 
-        qv_bf = tile("qv_bf", [P, Q, PACK], BF16)
+        qv_bf = tile("qv_bf", [P, Q, PACK], BF16, tag="qv_bf_then_f1b")
         for u in range(2):
             qv_ps = ps.tile([P, 2, Q], F32, name=f"qv_ps{u}", tag=f"qv_b_c{u}")
             for e in range(2):
@@ -129,6 +127,9 @@ def tile_attend_fanout_sidethree_kernel(tc, states, wq_words, wq_scales, cache_w
         qv_w = tile("qv_w", [P, Q], U32)
         qv_plane = tile("qv_plane", [P, Q], U8)
         nc.vector.quantize_mx(out=qv_w[:].bitcast(FP8X4), scales=qv_plane[:], in_=qv_bf[:].rearrange("p q t -> p (q t)"))
+
+        f1b = tile("f1b", [P, U], F32, tag="qv_bf_then_f1b")
+        nc.vector.memset(f1b[:], 0.0)
 
         a = tile("a", [P, T], F32)
         a_ps = []

from contextlib import ExitStack

import concourse.mybir as mybir

D, K, T, U, X, I, Q = 512, 512, 1024, 1024, 1024, 512, 128
FLOPS = 2 * Q * (D * K + K * T + K * U + D * X)

F32 = mybir.dt.float32
BF16 = mybir.dt.bfloat16
I32 = mybir.dt.int32
U32 = mybir.dt.uint32
U16 = mybir.dt.uint16
U8 = mybir.dt.uint8
FP8X4 = mybir.dt.float8_e4m3fn_x4
FP4X4 = mybir.dt.float4_e2m1fn_x4
COPY = mybir.ActivationFunctionType.Copy
ADD = mybir.AluOpType.add
SUB = mybir.AluOpType.subtract
MAX = mybir.AluOpType.max

P = 128
PACK = 4
BANK = 512
A_EDGES = (0, 256, 512, 768, 896, 1024)
A_ON_VECTOR = (0, 2)
AA_SPLIT = 704
HALF = I // 2
Q_VEC = 80
PER_COL = 16


def tile_attend_fanout_sidethree_kernel(tc, states, wq_words, wq_scales, cache_words, cache_scales, draft_words,
                                         draft_scales, arch_words, arch_scales, offs, offs2, offs3, offs4, offs5,
                                         offs6, offs7, out):
    nc = tc.nc
    with ExitStack() as ctx:
        sb = ctx.enter_context(tc.tile_pool(name="sb", bufs=1))
        ps = ctx.enter_context(tc.psum_pool(name="ps", bufs=1))

        def tile(name, shape, dtype, tag=None):
            return sb.tile(shape, dtype, name=name, tag=tag or name, align_bytes=64)

        def load_words(name, words, tag=None):
            t = tile(name, [P, words.shape[2]], U32, tag)
            nc.sync.dma_start(t[:].bitcast(I32), words[0].rearrange("p n t -> p (n t)").bitcast(I32))
            return t

        def zeroed_plane(name, width, tag=None):
            t = tile(name, [P, width], U8, tag)
            nc.vector.memset(t[:].bitcast(I32), 0)
            return t

        def load_plane(plane, scales):
            rows = scales[0].rearrange("(g r) n -> r g n", r=4)
            for r in range(4):
                nc.sync.dma_start(plane[r:P:32, :].bitcast(I32), rows[r].bitcast(I32))

        def load_list(name, lst):
            t = sb.tile([P, I // PER_COL], U16, name=name)
            nc.sync.dma_start(t[:], lst)
            return t

        def entries(lst, lo, hi):
            return lst[:, lo // PER_COL:hi // PER_COL]

        wq_plane_raw = zeroed_plane("wq_plane_raw", K)
        cache_plane = zeroed_plane("cache_plane", T)
        draft_plane = zeroed_plane("draft_plane", U, tag="draft_plane_then_f3")
        arch_plane = zeroed_plane("arch_plane", X)
        f1 = tile("f1", [P, U], F32)
        nc.vector.memset(f1[:], 0.0)

        st_raw = tile("st_raw", [P, PACK, Q], F32)
        nc.sync.dma_start(st_raw[:], states.rearrange("(p j) q -> p j q", j=PACK))
        wq_src = wq_words[0].rearrange("p n t -> p (n t)").bitcast(I32)
        wq_raw = []
        for h in range(2):
            half = tile(f"wq_raw{h}", [P, K // 2], U32)
            nc.sync.dma_start(half[:].bitcast(I32), wq_src[:, h * (K // 2):(h + 1) * (K // 2)])
            wq_raw.append(half)
            if h == 0:
                load_plane(wq_plane_raw, wq_scales)
        cache_w = load_words("cache_w", cache_words)
        load_plane(cache_plane, cache_scales)
        l1 = load_list("l1", offs)
        l2 = load_list("l2", offs2)
        l3 = load_list("l3", offs3)
        draft_w = tile("draft_w", [P, 2 * U], U8, tag="draft_w_then_f2")
        nc.sync.dma_start(draft_w[:].bitcast(I32), draft_words[0].bitcast(I32))
        load_plane(draft_plane, draft_scales)
        l4 = load_list("l4", offs4)
        l5 = load_list("l5", offs5)
        arch_w = load_words("arch_w", arch_words)
        load_plane(arch_plane, arch_scales)
        l7 = load_list("l7", offs7)
        l6 = load_list("l6", offs6)

        st_bf = tile("st_bf", [P, Q, PACK], BF16)
        nc.vector.tensor_copy(st_bf[:, 0:Q_VEC, :].rearrange("p (c i) j -> p c j i", i=4),
                              st_raw[:, :, 0:Q_VEC].rearrange("p j (c i) -> p c j i", i=4))
        nc.scalar.activation(st_bf[:, Q_VEC:Q, :].rearrange("p (c i) j -> p c j i", i=4),
                             st_raw[:, :, Q_VEC:Q].rearrange("p j (c i) -> p c j i", i=4), COPY)
        st_w = tile("st_w", [P, Q], U32)
        st_plane = tile("st_plane", [P, Q], U8)
        nc.vector.quantize_mx(out=st_w[:].bitcast(FP8X4), scales=st_plane[:], in_=st_bf[:].rearrange("p q j -> p (q j)"))

        wq_w = tile("wq_w", [P, K], U32)
        for h, places in ((0, slice(0, 4)), (1, slice(0, 2)), (1, slice(2, 4))):
            nc.scalar.copy(wq_w[:].rearrange("p (t m) -> p m t", t=PACK)[:, h * (P // 2):(h + 1) * (P // 2), places],
                           wq_raw[h][:].rearrange("p (m t) -> p m t", t=PACK)[:, :, places])
        wq_plane = tile("wq_plane", [P, K], U8)
        for u in range(2):
            nc.vector.tensor_copy(wq_plane[:].rearrange("p (t m) -> p t m", t=PACK)[:, 2 * u:2 * u + 2, :],
                                  wq_plane_raw[:].rearrange("p (m t) -> p t m", t=PACK)[:, 2 * u:2 * u + 2, :])

        qv_bf = tile("qv_bf", [P, Q, PACK], BF16, tag="qv_bf_then_f1b")
        for u in range(2):
            qv_ps = ps.tile([P, 2, Q], F32, name=f"qv_ps{u}", tag=f"qv_b_c{u}")
            for e in range(2):
                cols = slice((2 * u + e) * P, (2 * u + e + 1) * P)
                nc.tensor.matmul_mx(out=qv_ps[:, e, :], lhsT=wq_w[:, cols].bitcast(FP8X4), lhsT_scale=wq_plane[:, cols],
                                    rhs=st_w[:].bitcast(FP8X4), rhs_scale=st_plane[:], start=True, stop=True)
            if u == 0:
                nc.vector.tensor_copy(qv_bf[:, :, 0:2], qv_ps[:].rearrange("p e q -> p q e"))
            else:
                nc.scalar.copy(qv_bf[:, :, 2:4], qv_ps[:].rearrange("p e q -> p q e"))
        qv_w = tile("qv_w", [P, Q], U32)
        qv_plane = tile("qv_plane", [P, Q], U8)
        nc.vector.quantize_mx(out=qv_w[:].bitcast(FP8X4), scales=qv_plane[:], in_=qv_bf[:].rearrange("p q t -> p (q t)"))

        f1b = tile("f1b", [P, U], F32, tag="qv_bf_then_f1b")
        nc.vector.memset(f1b[:], 0.0)

        a = tile("a", [P, T], F32)
        a_ps = []
        for n in range(len(A_EDGES) - 1):
            cols = slice(A_EDGES[n], A_EDGES[n + 1])
            bank = ps.tile([P, cols.stop - cols.start], F32, name=f"a_ps{n}")
            nc.tensor.matmul_mx(out=bank[:], lhsT=qv_w[:].bitcast(FP8X4), lhsT_scale=qv_plane[:],
                                rhs=cache_w[:, cols].bitcast(FP8X4), rhs_scale=cache_plane[:, cols],
                                start=True, stop=True)
            if n in A_ON_VECTOR:
                nc.vector.tensor_copy(a[:, cols], bank[:])
            else:
                nc.scalar.copy(a[:, cols], bank[:])
            a_ps.append(bank)

        def scatter(window, lst, src, lo, hi):
            nc.scalar.activation(window[:].indirect(entries(lst, lo, hi)), src[:, lo:hi], COPY)

        ga = tile("ga", [P, I], F32)
        nc.vector.tensor_copy(ga[:, 0:HALF], a[:].indirect(entries(l1, 0, HALF)))
        scatter(f1, l2, ga, 0, HALF)
        nc.vector.tensor_copy(ga[:, HALF:I], a[:].indirect(entries(l1, HALF, I)))
        scatter(f1b, l2, ga, HALF, I)

        bb_half = tile("bb_half", [P, U], F32)
        for n in range(U // BANK):
            cols = slice(n * BANK, (n + 1) * BANK)
            b_ps = ps.tile([P, BANK], F32, name=f"b_ps{n}", tag=f"qv_b_c{n}")
            nc.tensor.matmul_mx(out=b_ps[:], lhsT=qv_w[:].bitcast(FP8X4), lhsT_scale=qv_plane[:],
                                rhs=draft_w[:, 2 * n * BANK:2 * (n + 1) * BANK].bitcast(FP4X4),
                                rhs_scale=draft_plane[:, cols], start=True, stop=True)
            nc.vector.tensor_tensor(bb_half[:, cols], b_ps[:], f1[:, cols], ADD)
        f2 = tile("f2", [P, X], F32, tag="draft_w_then_f2")
        nc.gpsimd.memset(f2[:], 0.0)
        f3 = tile("f3", [P, T], F32, tag="draft_plane_then_f3")
        nc.gpsimd.memset(f3[:], 0.0)
        scatter(f2, l3, ga, 0, I)
        bb = tile("bb", [P, U], F32, tag="bb_cc_aa")
        nc.vector.tensor_tensor(bb[:], bb_half[:], f1b[:], ADD)
        gb = tile("gb", [P, I], F32)
        nc.vector.tensor_copy(gb[:], bb[:].indirect(l4[:]))
        scatter(f3, l5, gb, 0, I)

        cc = tile("cc", [P, X], F32, tag="bb_cc_aa")
        for n in range(X // BANK):
            cols = slice(n * BANK, (n + 1) * BANK)
            c_ps = ps.tile([P, BANK], F32, name=f"c_ps{n}", tag=f"qv_b_c{n}")
            nc.tensor.matmul_mx(out=c_ps[:], lhsT=st_w[:].bitcast(FP8X4), lhsT_scale=st_plane[:],
                                rhs=arch_w[:, cols].bitcast(FP8X4), rhs_scale=arch_plane[:, cols],
                                start=True, stop=True)
            nc.vector.tensor_tensor(cc[:, cols], c_ps[:], f2[:, cols], SUB)
        gc = tile("gc", [P, I], F32)
        nc.vector.tensor_copy(gc[:], cc[:].indirect(l7[:]))

        aa = tile("aa", [P, T], F32, tag="bb_cc_aa")
        for n, bank in enumerate(a_ps):
            lo, hi = A_EDGES[n], min(A_EDGES[n + 1], AA_SPLIT)
            if lo < hi:
                nc.vector.tensor_tensor(aa[:, lo:hi], bank[:, 0:hi - lo], f3[:, lo:hi], SUB)
        nc.gpsimd.tensor_tensor(aa[:, AA_SPLIT:T], a[:, AA_SPLIT:T], f3[:, AA_SPLIT:T], SUB)

        gaa = tile("gaa", [P, I], F32)
        nc.vector.tensor_copy(gaa[:, 0:HALF], aa[:].indirect(entries(l6, 0, HALF)))
        nc.scalar.activation(gaa[:, HALF:I], aa[:].indirect(entries(l6, HALF, I)), COPY)
        for name, cols, tag in (("y_hi", slice(HALF, I), None), ("y_lo", slice(0, HALF), "bb_cc_aa")):
            y = tile(name, [P, HALF], F32, tag)
            nc.vector.tensor_tensor(y[:], gaa[:, cols], gc[:, cols], MAX)
            nc.sync.dma_start(out[:, cols], y[:])
